import numpy as np
import ml_dtypes


def mxq(x, axis, fmt="e4m3"):
    dtype, down = {"e4m3": (ml_dtypes.float8_e4m3fn, 7), "e5m2": (ml_dtypes.float8_e5m2, 14)}[fmt]
    v = np.moveaxis(np.asarray(x, np.float32).astype(ml_dtypes.bfloat16).astype(np.float64), axis, -1)
    blocks = v.reshape(v.shape[:-1] + (-1, 32))
    amax = np.abs(blocks).max(-1, keepdims=True)
    byte = np.maximum(np.where(amax > 0, np.frexp(amax)[1] - 1 + 127, 0) - down, 1)
    scale = np.exp2(byte - 127.0)
    codes = (blocks / scale).astype(np.float32).astype(dtype).astype(np.float64)
    return np.moveaxis((codes * scale).reshape(v.shape), -1, axis)


WIDE = False


def mx_kscale(k):
    if not WIDE:
        return np.ones(k)
    levels = np.array([10, -10, 5, -5, 0])
    if k % 512:
        return np.exp2(np.random.permutation(np.resize(levels, k // 32))).repeat(32)
    a = np.empty((k // 512, 16))
    for p in range(k // 512):
        a[p, :8] = np.random.permutation(np.resize(levels, 8))
        for g in range(8):
            far = levels[np.abs(levels - a[p, g]) >= 10]
            a[p, g + 8] = far[np.random.randint(len(far))]
    return np.exp2(a.ravel()).repeat(32)


BF16 = ml_dtypes.bfloat16


def bf(x):
    return np.asarray(x, np.float32).astype(BF16)


def f64(x):
    return np.asarray(x).astype(np.float64)


E2M1 = np.array([0.0, 0.5, 1.0, 1.5, 2.0, 3.0, 4.0, 6.0, -0.0, -0.5, -1.0, -1.5, -2.0, -3.0, -4.0, -6.0])


def pack_weight(w, fmt):
    k, n = w.shape
    w = f64(bf(w)).reshape(k // 32, 32, n)
    amax = np.abs(w).max(1)
    if fmt == "e4m3":
        byte = np.frexp(amax)[1] - 1 + 127 - 7
    else:
        mant, ex = np.frexp(amax / 6.0)
        byte = np.where(mant > 0.5, ex, ex - 1) + 127
    byte = np.clip(np.where(amax > 0, byte, 1), 1, 254)
    scaled = (w * np.exp2(127.0 - byte)[:, None, :]).reshape(k, n).astype(np.float32)
    by_word = np.ascontiguousarray(scaled.reshape(k // 512, 128, 4, n).transpose(0, 1, 3, 2))
    if fmt == "e4m3":
        words = by_word.astype(ml_dtypes.float8_e4m3fn).view(np.uint8)
    else:
        c = by_word.astype(ml_dtypes.float4_e2m1fn).view(np.uint8) & 0xF
        words = c[..., 0::2] | (c[..., 1::2] << 4)
    return np.ascontiguousarray(words), np.ascontiguousarray(byte.astype(np.uint8).reshape(k // 512, 16, n))


def unpack_weight(words, scales, fmt):
    g, p, n, _ = words.shape
    if fmt == "e4m3":
        vals = np.ascontiguousarray(words).view(ml_dtypes.float8_e4m3fn).astype(np.float64)
    else:
        nib = np.empty((g, p, n, 4), np.uint8)
        nib[..., 0::2] = words & 0xF
        nib[..., 1::2] = words >> 4
        vals = E2M1[nib]
    vals = vals * np.repeat(np.exp2(scales.astype(np.float64) - 127.0), 8, axis=1)[..., None]
    return vals.transpose(0, 1, 3, 2).reshape(g * 512, n)
def pack4(w):
    words, scales = pack_weight(w, "e2m1")
    return words.reshape(words.shape[0], 128, -1), scales


def unpack4(words, scales):
    return unpack_weight(words.reshape(words.shape[0], 128, -1, 2), scales, "e2m1")


B, T, K, A = 64, 32, 1024, 512


def setup_inputs():
    s = mx_kscale(K)
    w1 = np.random.standard_normal((K, A)) * np.sqrt(2 / K) / s[:, None]
    w2 = np.random.standard_normal((K, A)) * np.sqrt(2 / K) / s[:, None]
    w3 = np.random.standard_normal((K, A)) * np.sqrt(2 / K) / s[:, None]
    w1_words, w1_scales = pack4(w1)
    w2_words, w2_scales = pack_weight(w2, "e4m3")
    return {"psi": bf(np.random.standard_normal((B, K)) * s),
            "emb": bf(np.random.standard_normal((T, K))),
            "w1_words": w1_words, "w1_scales": w1_scales,
            "w2_words": w2_words, "w2_scales": w2_scales,
            "w3": bf(w3),
            "eps": bf(np.random.standard_normal((B, A))),
            "bias": bf(0.4 * np.random.standard_normal((A,)))}


def reference(psi, emb, w1_words, w1_scales, w2_words, w2_scales, w3, eps, bias):
    phi = np.maximum(f64(emb), 0.0)
    z = (f64(psi)[:, None, :] * phi[None, :, :]).reshape(B * T, K)
    zq = mxq(z, 1, "e4m3")
    prior = zq @ unpack4(w1_words, w1_scales)
    sigma = zq @ unpack_weight(w2_words, w2_scales, "e4m3")
    mean = zq @ mxq(f64(w3), 0, "e4m3")
    noise = sigma.reshape(B, T, A) * f64(eps)[:, None, :]
    return mean.reshape(B, T, A) + prior.reshape(B, T, A) + noise + f64(bias)

@@ -1,0 +1,236 @@
+from contextlib import ExitStack
+
+import concourse.mybir as mybir
+from concourse.masks import make_identity
+
+STATES, FRACTIONS, K, ACTIONS = 64, 32, 1024, 512
+FLOPS = 3 * 2 * STATES * FRACTIONS * K * ACTIONS
+
+F32 = mybir.dt.float32
+BF16 = mybir.dt.bfloat16
+U32 = mybir.dt.uint32
+I32 = mybir.dt.int32
+U8 = mybir.dt.uint8
+E4M3 = mybir.dt.float8_e4m3fn_x4
+E2M1 = mybir.dt.float4_e2m1fn_x4
+ADD = mybir.AluOpType.add
+MULT = mybir.AluOpType.mult
+
+P = 128
+G = K // 512
+H = P // STATES
+TILES = FRACTIONS // H
+
+
+def tile_implicit_quantile_head_s10_kernel(
+    tc, psi, emb, w1_words, w1_scales, w2_words, w2_scales, w3, eps, bias, out
+):
+    nc = tc.nc
+    with ExitStack() as ctx:
+        keep = ctx.enter_context(tc.tile_pool(name="keep", bufs=1))
+        zpool = ctx.enter_context(tc.tile_pool(name="zpool", bufs=3))
+        cpool = ctx.enter_context(tc.tile_pool(name="cpool", bufs=TILES))
+        epi = ctx.enter_context(tc.tile_pool(name="epi", bufs=6))
+        psum = ctx.enter_context(tc.psum_pool(name="psum", bufs=4))
+        ctx.enter_context(tc.manual_schedule())
+
+        rows = keep.tile([P, K], BF16, align_bytes=64, name="rows")
+        planes = keep.tile([P, 2 * G, ACTIONS], U8, align_bytes=64, name="planes")
+        w2 = keep.tile([P, G, ACTIONS], U32, align_bytes=64, name="w2c")
+        w1 = keep.tile([P, G, 2 * ACTIONS], U8, align_bytes=64, name="w1c")
+        w3_raw = keep.tile([P, G, 4, ACTIONS], BF16, align_bytes=64, name="w3_raw")
+        w3_grouped = keep.tile([P, G, ACTIONS, 4], BF16, align_bytes=64, name="w3_grouped")
+        w3_codes = keep.tile([P, G, ACTIONS], U32, align_bytes=64, name="w3_codes")
+        w3_scales = keep.tile([P, G, ACTIONS], U8, align_bytes=64, name="w3_scales")
+        eps_rows = keep.tile([P, ACTIONS], BF16, align_bytes=64, name="eps_rows")
+        bias_rows = keep.tile([P, ACTIONS], BF16, align_bytes=64, name="bias_rows")
+        ident = keep.tile([P, P], F32, align_bytes=64, name="ident")
+        psi_t = keep.tile([P, G, STATES, H, 4], BF16, align_bytes=64, name="psi_t")
+        phi_t = keep.tile([P, G, TILES, H, 4], BF16, align_bytes=64, name="phi_t")
+
+        nc.sync.dma_start(out=rows[0:STATES, :], in_=psi)
+        nc.sync.dma_start(out=rows[STATES : STATES + FRACTIONS, :], in_=emb)
+        nc.vector.memset(planes[:].rearrange("p a n -> p (a n)").bitcast(I32), 0)
+        nc.vector.memset(rows[STATES + FRACTIONS : P, :].bitcast(I32), 0)
+        make_identity(nc, ident[:])
+        for h in range(H):
+            nc.gpsimd.dma_start(out=eps_rows[h:P:H, :], in_=eps)
+
+        def load_scales(src, at):
+            by_row = src.rearrange("g (q r) n -> r q g n", r=4)
+            for r in range(4):
+                nc.sync.dma_start(
+                    out=planes[r:P:32, at : at + G, :].bitcast(I32), in_=by_row[r].bitcast(I32)
+                )
+
+        load_scales(w2_scales, G)
+        nc.sync.dma_start(
+            out=w2[:].bitcast(I32), in_=w2_words.rearrange("g p n t -> p g (n t)").bitcast(I32)
+        )
+        load_scales(w1_scales, 0)
+        nc.sync.dma_start(out=w1[:].bitcast(I32), in_=w1_words.rearrange("g p b -> p g b").bitcast(I32))
+        for g in range(G):
+            nc.sync.dma_start(
+                out=w3_raw[:, g], in_=w3[512 * g : 512 * (g + 1), :].rearrange("(p j) n -> p j n", j=4)
+            )
+        nc.sync.dma_start(out=bias_rows[:], in_=bias.partition_broadcast(P))
+
+        words = rows[:].bitcast(F32)
+        for g in range(G):
+            turned = psum.tile([P, ACTIONS], F32, tag=("pb", "pa")[g], name="turned")
+            for u in range(2):
+                nc.tensor.transpose(
+                    turned[:, P * u : P * (u + 1)], words[:, 256 * g + u : 256 * (g + 1) : 2], ident[:]
+                )
+            pairs = turned[:, 0 : 2 * P].rearrange("p (u r) -> p r u", u=2)
+            nc.scalar.copy(
+                out=psi_t[:, g].rearrange("p i h t -> p (i h t)").bitcast(F32).rearrange("p (i h u) -> p i h u", h=H, u=2),
+                in_=pairs[:, 0:STATES, :].unsqueeze(2).to_broadcast([P, STATES, H, 2]),
+            )
+            halves = turned[:, 0 : 2 * P].bitcast(BF16).rearrange("p (u r e) -> p r u e", u=2, e=2)
+            for h in range(H):
+                first = STATES + TILES * h
+                nc.vector.tensor_scalar_max(
+                    phi_t[:, g, :, h, :].rearrange("p s (u e) -> p s u e", e=2),
+                    halves[:, first : first + TILES, :, :],
+                    0.0,
+                )
+
+        for g in range(G):
+            for n in range(0, ACTIONS, 256):
+                nc.scalar.copy(
+                    out=w3_grouped[:, g, n : n + 256, :],
+                    in_=w3_raw[:, g, :, n : n + 256].rearrange("p j n -> p n j"),
+                )
+
+        def quantize_w3(g):
+            nc.vector.quantize_mx(
+                out=w3_codes[:, g, :].bitcast(E4M3),
+                scales=w3_scales[:, g, :],
+                in_=w3_grouped[:, g].rearrange("p n t -> p (n t)"),
+            )
+
+        z_of, codes_of, scales_of = {}, {}, {}
+        t1_of = {}
+        pb_of, pa_of = {}, {}
+
+        def zmul(first, count, g):
+            if g == 0:
+                z_of[first] = zpool.tile([P, G, count, STATES * H * 4], BF16, align_bytes=64, tag="z", name="z")
+            z = z_of[first]
+            nc.vector.tensor_tensor(
+                out=z[:, g].rearrange("p s (i x) -> p s i x", x=H * 4),
+                in0=psi_t[:, g].rearrange("p i h t -> p i (h t)").unsqueeze(1).to_broadcast([P, count, STATES, H * 4]),
+                in1=phi_t[:, g, first : first + count]
+                .rearrange("p s h t -> p s (h t)")
+                .unsqueeze(2)
+                .to_broadcast([P, count, STATES, H * 4]),
+                op=MULT,
+            )
+
+        def quant(first, count, split=False):
+            z = z_of.pop(first)
+            codes = cpool.tile([P, G, count, P], U32, align_bytes=64, tag="codes", name="codes")
+            scales = cpool.tile([P, G, count, P], U8, align_bytes=64, tag="scales", name="scales")
+            if split:
+                for g in range(G):
+                    nc.vector.quantize_mx(
+                        out=codes[:, g].rearrange("p s r -> p (s r)").bitcast(E4M3),
+                        scales=scales[:, g].rearrange("p s r -> p (s r)"),
+                        in_=z[:, g].rearrange("p s x -> p (s x)"),
+                    )
+            else:
+                nc.vector.quantize_mx(
+                    out=codes[:].rearrange("p g s r -> p (g s r)").bitcast(E4M3),
+                    scales=scales[:].rearrange("p g s r -> p (g s r)"),
+                    in_=z[:].rearrange("p g s x -> p (g s x)"),
+                )
+            for c in range(count):
+                codes_of[first + c] = codes[:, :, c, :]
+                scales_of[first + c] = scales[:, :, c, :]
+
+        def product(bank, s, moving, moving_scales, start, stop):
+            for g in range(G):
+                nc.tensor.matmul_mx(
+                    out=bank[:],
+                    lhsT=codes_of[s][:, g, :].bitcast(E4M3),
+                    lhsT_scale=scales_of[s][:, g, :],
+                    rhs=moving(g),
+                    rhs_scale=moving_scales(g),
+                    start=start and g == 0,
+                    stop=stop and g == G - 1,
+                )
+
+        def mm_noise(s):
+            pb_of[s] = psum.tile([P, ACTIONS], F32, tag="pb", name="pb")
+            product(pb_of[s], s, lambda g: w2[:, g, :].bitcast(E4M3), lambda g: planes[:, G + g, :], True, True)
+
+        def mm_prior(s):
+            pa_of[s] = psum.tile([P, ACTIONS], F32, tag="pa", name="pa")
+            product(pa_of[s], s, lambda g: w1[:, g, :].bitcast(E2M1), lambda g: planes[:, g, :], True, False)
+
+        def mm_mean(s):
+            product(pa_of[s], s, lambda g: w3_codes[:, g, :].bitcast(E4M3), lambda g: w3_scales[:, g, :], False, True)
+
+        def noise(s):
+            t1 = epi.tile([P, ACTIONS], F32, tag="t1", name="t1")
+            nc.vector.tensor_tensor(out=t1[:], in0=pb_of.pop(s)[:], in1=eps_rows[:], op=MULT)
+            t2 = epi.tile([P, ACTIONS], F32, tag="t2", name="t2")
+            nc.gpsimd.tensor_tensor(out=t2[:], in0=t1[:], in1=bias_rows[:], op=ADD)
+            t1_of[s] = t2
+
+        by_tile = out.rearrange("i (h s) a -> s (i h) a", h=H)
+
+        def finish(s):
+            o = epi.tile([P, ACTIONS], F32, tag="o", name="o")
+            nc.vector.tensor_tensor(out=o[:], in0=pa_of.pop(s)[:], in1=t1_of.pop(s)[:], op=ADD)
+            nc.sync.dma_start(out=by_tile[s], in_=o[:])
+
+        zmul(0, 1, 0)
+        zmul(0, 1, 1)
+        quant(0, 1, split=True)
+        mm_noise(0)
+        mm_prior(0)
+        zmul(1, 1, 0)
+        zmul(1, 1, 1)
+        zmul(2, 2, 0)
+        quant(1, 1)
+        mm_noise(1)
+        mm_prior(1)
+        zmul(2, 2, 1)
+        noise(0)
+        quant(2, 2)
+        mm_noise(2)
+        mm_prior(2)
+        mm_noise(3)
+        mm_prior(3)
+        noise(1)
+        zmul(4, 2, 0)
+        quantize_w3(0)
+        zmul(4, 2, 1)
+        noise(2)
+        quant(4, 2)
+        noise(3)
+        quantize_w3(1)
+        for p in range(TILES // 2):
+            a, b = 2 * p, 2 * p + 1
+            more_z = p + 3 < TILES // 2
+            more_mm = p + 2 < TILES // 2
+            mm_mean(a)
+            mm_mean(b)
+            if more_mm:
+                mm_noise(a + 4)
+                mm_noise(b + 4)
+            if more_z:
+                zmul(a + 6, 2, 0)
+            finish(a)
+            if more_z:
+                zmul(a + 6, 2, 1)
+            finish(b)
+            if more_z:
+                quant(a + 6, 2)
+            if more_mm:
+                mm_prior(a + 4)
+                mm_prior(b + 4)
+                noise(a + 4)
+                noise(b + 4)

@@ -15,11 +15,17 @@ E4M3 = mybir.dt.float8_e4m3fn_x4
 E2M1 = mybir.dt.float4_e2m1fn_x4
 ADD = mybir.AluOpType.add
 MULT = mybir.AluOpType.mult
+IDENTITY = mybir.ActivationFunctionType.Identity
 
 P = 128
 G = K // 512
-H = P // STATES
-TILES = FRACTIONS // H
+ROWS = 512
+BLOCKS = STATES * FRACTIONS // ROWS
+BS = STATES // BLOCKS
+AT = ACTIONS // P
+RT = ROWS // P
+H = P // BS
+LAST = BLOCKS - 1
 
 
 def tile_implicit_quantile_head_s10_kernel(
@@ -28,13 +34,19 @@ def tile_implicit_quantile_head_s10_kernel(
     nc = tc.nc
     with ExitStack() as ctx:
         keep = ctx.enter_context(tc.tile_pool(name="keep", bufs=1))
-        zpool = ctx.enter_context(tc.tile_pool(name="zpool", bufs=3))
-        cpool = ctx.enter_context(tc.tile_pool(name="cpool", bufs=TILES))
-        epi = ctx.enter_context(tc.tile_pool(name="epi", bufs=6))
-        psum = ctx.enter_context(tc.psum_pool(name="psum", bufs=4))
+        zpool = ctx.enter_context(tc.tile_pool(name="zpool", bufs=4))
+        cpool = ctx.enter_context(tc.tile_pool(name="cpool", bufs=BLOCKS))
+        epi = ctx.enter_context(tc.tile_pool(name="epi", bufs=5))
+        opool = ctx.enter_context(tc.tile_pool(name="opool", bufs=2))
+        psum = ctx.enter_context(tc.psum_pool(name="psum", bufs=8))
         ctx.enter_context(tc.manual_schedule())
 
+        def bank():
+            t = psum.tile([P, 512], F32, tag="bank", name="bank")
+            return t
+
         rows = keep.tile([P, K], BF16, align_bytes=64, name="rows")
+        erows = keep.tile([P, ACTIONS], BF16, align_bytes=64, name="erows")
         planes = keep.tile([P, 2 * G, ACTIONS], U8, align_bytes=64, name="planes")
         w2 = keep.tile([P, G, ACTIONS], U32, align_bytes=64, name="w2c")
         w1 = keep.tile([P, G, 2 * ACTIONS], U8, align_bytes=64, name="w1c")
@@ -45,16 +57,24 @@ def tile_implicit_quantile_head_s10_kernel(
         eps_rows = keep.tile([P, ACTIONS], BF16, align_bytes=64, name="eps_rows")
         bias_rows = keep.tile([P, ACTIONS], BF16, align_bytes=64, name="bias_rows")
         ident = keep.tile([P, P], F32, align_bytes=64, name="ident")
-        psi_t = keep.tile([P, G, STATES, H, 4], BF16, align_bytes=64, name="psi_t")
-        phi_t = keep.tile([P, G, TILES, H, 4], BF16, align_bytes=64, name="phi_t")
+        ident_b = keep.tile([P, P], BF16, align_bytes=64, name="ident_b")
+        psi_t = keep.tile([P, G, STATES, 4], BF16, align_bytes=64, name="psi_t")
+        phi_t = keep.tile([P, G, FRACTIONS, 4], BF16, align_bytes=64, name="phi_t")
+        eps_t = keep.tile([P, AT, STATES + 1], F32, align_bytes=64, name="eps_t")
+        warm = keep.tile([P, 1], F32, align_bytes=64, name="warm")
 
         nc.sync.dma_start(out=rows[0:STATES, :], in_=psi)
         nc.sync.dma_start(out=rows[STATES : STATES + FRACTIONS, :], in_=emb)
+        nc.sync.dma_start(out=erows[0:STATES, :], in_=eps)
+        nc.vector.memset(warm[:], 0.0)
+        nc.scalar.activation(warm[:], warm[:], IDENTITY)
         nc.vector.memset(planes[:].rearrange("p a n -> p (a n)").bitcast(I32), 0)
         nc.vector.memset(rows[STATES + FRACTIONS : P, :].bitcast(I32), 0)
+        nc.vector.memset(erows[STATES:P, :].bitcast(I32), 0)
         make_identity(nc, ident[:])
+        make_identity(nc, ident_b[:])
         for h in range(H):
-            nc.gpsimd.dma_start(out=eps_rows[h:P:H, :], in_=eps)
+            nc.gpsimd.dma_start(out=eps_rows[h:P:H, :], in_=eps[BS * LAST : STATES, :])
 
         def load_scales(src, at):
             by_row = src.rearrange("g (q r) n -> r q g n", r=4)
@@ -63,6 +83,7 @@ def tile_implicit_quantile_head_s10_kernel(
                     out=planes[r:P:32, at : at + G, :].bitcast(I32), in_=by_row[r].bitcast(I32)
                 )
 
+        nc.sync.dma_start(out=erows[STATES : STATES + 1, :], in_=bias.unsqueeze(0))
         load_scales(w2_scales, G)
         nc.sync.dma_start(
             out=w2[:].bitcast(I32), in_=w2_words.rearrange("g p n t -> p g (n t)").bitcast(I32)
@@ -77,31 +98,38 @@ def tile_implicit_quantile_head_s10_kernel(
 
         words = rows[:].bitcast(F32)
         for g in range(G):
-            turned = psum.tile([P, ACTIONS], F32, tag=("pb", "pa")[g], name="turned")
+            turned = bank()
             for u in range(2):
                 nc.tensor.transpose(
                     turned[:, P * u : P * (u + 1)], words[:, 256 * g + u : 256 * (g + 1) : 2], ident[:]
                 )
             pairs = turned[:, 0 : 2 * P].rearrange("p (u r) -> p r u", u=2)
             nc.scalar.copy(
-                out=psi_t[:, g].rearrange("p i h t -> p (i h t)").bitcast(F32).rearrange("p (i h u) -> p i h u", h=H, u=2),
-                in_=pairs[:, 0:STATES, :].unsqueeze(2).to_broadcast([P, STATES, H, 2]),
+                out=psi_t[:, g].rearrange("p i t -> p (i t)").bitcast(F32).rearrange("p (i u) -> p i u", u=2),
+                in_=pairs[:, 0:STATES, :],
             )
             halves = turned[:, 0 : 2 * P].bitcast(BF16).rearrange("p (u r e) -> p r u e", u=2, e=2)
-            for h in range(H):
-                first = STATES + TILES * h
-                nc.vector.tensor_scalar_max(
-                    phi_t[:, g, :, h, :].rearrange("p s (u e) -> p s u e", e=2),
-                    halves[:, first : first + TILES, :, :],
-                    0.0,
-                )
+            nc.vector.tensor_scalar_max(
+                phi_t[:, g].rearrange("p j (u e) -> p j u e", e=2),
+                halves[:, STATES : STATES + FRACTIONS, :, :],
+                0.0,
+            )
 
-        for g in range(G):
-            for n in range(0, ACTIONS, 256):
-                nc.scalar.copy(
-                    out=w3_grouped[:, g, n : n + 256, :],
-                    in_=w3_raw[:, g, :, n : n + 256].rearrange("p j n -> p n j"),
-                )
+        eturned = psum.tile([P, AT, P], BF16, tag="bank", name="eturned")
+        for at in range(AT):
+            nc.tensor.transpose(eturned[:, at, :], erows[:, P * at : P * (at + 1)], ident_b[:])
+        nc.scalar.copy(out=eps_t[:], in_=eturned[:, :, 0 : STATES + 1])
+
+        def interleave_w3(copy, g, half):
+            n = 256 * half
+            copy(
+                out=w3_grouped[:, g, n : n + 256, :],
+                in_=w3_raw[:, g, :, n : n + 256].rearrange("p j n -> p n j"),
+            )
+
+        interleave_w3(nc.scalar.copy, 0, 0)
+        interleave_w3(nc.scalar.copy, 0, 1)
+        interleave_w3(nc.scalar.copy, 1, 0)
 
         def quantize_w3(g):
             nc.vector.quantize_mx(
@@ -111,126 +139,183 @@ def tile_implicit_quantile_head_s10_kernel(
             )
 
         z_of, codes_of, scales_of = {}, {}, {}
-        t1_of = {}
-        pb_of, pa_of = {}, {}
 
-        def zmul(first, count, g):
+        def zmul(b, g):
+            z = zpool.tile([P, ROWS * 4], BF16, align_bytes=64, tag="z", name="z")
+            z_of[b, g] = z
+            own = psi_t[:, g, BS * b : BS * (b + 1), :]
+            if b < LAST:
+                shape = [P, BS, FRACTIONS, 4]
+                nc.vector.tensor_tensor(
+                    out=z[:].rearrange("p (i j t) -> p i j t", j=FRACTIONS, t=4),
+                    in0=own.unsqueeze(2).to_broadcast(shape),
+                    in1=phi_t[:, g].unsqueeze(1).to_broadcast(shape),
+                    op=MULT,
+                )
+            else:
+                shape = [P, BS, H, 4]
+                for s in range(RT):
+                    nc.vector.tensor_tensor(
+                        out=z[:, 512 * s : 512 * (s + 1)].rearrange("p (i h t) -> p i h t", h=H, t=4),
+                        in0=own.unsqueeze(2).to_broadcast(shape),
+                        in1=phi_t[:, g, s:FRACTIONS:RT, :].unsqueeze(1).to_broadcast(shape),
+                        op=MULT,
+                    )
+
+        def quant(b, g):
             if g == 0:
-                z_of[first] = zpool.tile([P, G, count, STATES * H * 4], BF16, align_bytes=64, tag="z", name="z")
-            z = z_of[first]
-            nc.vector.tensor_tensor(
-                out=z[:, g].rearrange("p s (i x) -> p s i x", x=H * 4),
-                in0=psi_t[:, g].rearrange("p i h t -> p i (h t)").unsqueeze(1).to_broadcast([P, count, STATES, H * 4]),
-                in1=phi_t[:, g, first : first + count]
-                .rearrange("p s h t -> p s (h t)")
-                .unsqueeze(2)
-                .to_broadcast([P, count, STATES, H * 4]),
-                op=MULT,
+                codes_of[b] = cpool.tile([P, G, ROWS], U32, align_bytes=64, tag="codes", name="codes")
+                scales_of[b] = cpool.tile([P, G, ROWS], U8, align_bytes=64, tag="scales", name="scales")
+            nc.vector.quantize_mx(
+                out=codes_of[b][:, g, :].bitcast(E4M3),
+                scales=scales_of[b][:, g, :],
+                in_=z_of.pop((b, g))[:],
             )
 
-        def quant(first, count, split=False):
-            z = z_of.pop(first)
-            codes = cpool.tile([P, G, count, P], U32, align_bytes=64, tag="codes", name="codes")
-            scales = cpool.tile([P, G, count, P], U8, align_bytes=64, tag="scales", name="scales")
-            if split:
-                for g in range(G):
-                    nc.vector.quantize_mx(
-                        out=codes[:, g].rearrange("p s r -> p (s r)").bitcast(E4M3),
-                        scales=scales[:, g].rearrange("p s r -> p (s r)"),
-                        in_=z[:, g].rearrange("p s x -> p (s x)"),
+        def weights(kind, g, at=None):
+            lo, hi = (0, ACTIONS) if at is None else (P * at, P * (at + 1))
+            if kind == 1:
+                return w1[:, g, 2 * lo : 2 * hi].bitcast(E2M1), planes[:, g, lo:hi]
+            if kind == 2:
+                return w2[:, g, lo:hi].bitcast(E4M3), planes[:, G + g, lo:hi]
+            return w3_codes[:, g, lo:hi].bitcast(E4M3), w3_scales[:, g, lo:hi]
+
+        def mm_turned(dst, kind, b, at, g, start, stop):
+            w, ws = weights(kind, g, at)
+            nc.tensor.matmul_mx(
+                out=dst[:],
+                lhsT=w,
+                lhsT_scale=ws,
+                rhs=codes_of[b][:, g, :].bitcast(E4M3),
+                rhs_scale=scales_of[b][:, g, :],
+                start=start,
+                stop=stop,
+            )
+
+        def mm_rows(dst, kind, s, g, start, stop):
+            w, ws = weights(kind, g)
+            nc.tensor.matmul_mx(
+                out=dst[:],
+                lhsT=codes_of[LAST][:, g, P * s : P * (s + 1)].bitcast(E4M3),
+                lhsT_scale=scales_of[LAST][:, g, P * s : P * (s + 1)],
+                rhs=w,
+                rhs_scale=ws,
+                start=start,
+                stop=stop,
+            )
+
+        def scale_noise(b, at, src):
+            t = epi.tile([P, ROWS], F32, tag="noise", name="noise")
+            for i in range(BS):
+                nc.scalar.activation(
+                    t[:, FRACTIONS * i : FRACTIONS * (i + 1)],
+                    src[:, FRACTIONS * i : FRACTIONS * (i + 1)],
+                    IDENTITY,
+                    bias=eps_t[:, at, STATES : STATES + 1],
+                    scale=eps_t[:, at, BS * b + i : BS * b + i + 1],
+                )
+            return t
+
+        sums_of = {}
+
+        def add_up(b, at, src, noise):
+            if at == 0:
+                sums_of[b] = opool.tile([P, AT, ROWS], F32, tag="sums", name="sums")
+            nc.vector.tensor_tensor(out=sums_of[b][:, at, :], in0=src[:], in1=noise[:], op=ADD)
+
+        out_rows = out.rearrange("i j a -> (i j) a")
+
+        def turn_back(b):
+            res = []
+            for r in range(RT):
+                dst = bank()
+                for at in range(AT):
+                    nc.tensor.transpose(
+                        dst[:, P * at : P * (at + 1)], sums_of[b][:, at, P * r : P * (r + 1)], ident[:]
                     )
-            else:
-                nc.vector.quantize_mx(
-                    out=codes[:].rearrange("p g s r -> p (g s r)").bitcast(E4M3),
-                    scales=scales[:].rearrange("p g s r -> p (g s r)"),
-                    in_=z[:].rearrange("p g s x -> p (g s x)"),
-                )
-            for c in range(count):
-                codes_of[first + c] = codes[:, :, c, :]
-                scales_of[first + c] = scales[:, :, c, :]
+                res.append(dst)
+            return res
 
-        def product(bank, s, moving, moving_scales, start, stop):
-            for g in range(G):
-                nc.tensor.matmul_mx(
-                    out=bank[:],
-                    lhsT=codes_of[s][:, g, :].bitcast(E4M3),
-                    lhsT_scale=scales_of[s][:, g, :],
-                    rhs=moving(g),
-                    rhs_scale=moving_scales(g),
-                    start=start and g == 0,
-                    stop=stop and g == G - 1,
-                )
+        def store(b, banks):
+            for r in range(RT):
+                o = epi.tile([P, ACTIONS], F32, tag="o", name="o")
+                (nc.scalar.copy, nc.vector.tensor_copy)[r % 2](out=o[:], in_=banks[r][:])
+                lo = ROWS * b + P * r
+                nc.sync.dma_start(out=out_rows[lo : lo + P, :], in_=o[:])
 
-        def mm_noise(s):
-            pb_of[s] = psum.tile([P, ACTIONS], F32, tag="pb", name="pb")
-            product(pb_of[s], s, lambda g: w2[:, g, :].bitcast(E4M3), lambda g: planes[:, G + g, :], True, True)
-
-        def mm_prior(s):
-            pa_of[s] = psum.tile([P, ACTIONS], F32, tag="pa", name="pa")
-            product(pa_of[s], s, lambda g: w1[:, g, :].bitcast(E2M1), lambda g: planes[:, g, :], True, False)
-
-        def mm_mean(s):
-            product(pa_of[s], s, lambda g: w3_codes[:, g, :].bitcast(E4M3), lambda g: w3_scales[:, g, :], False, True)
-
-        def noise(s):
-            t1 = epi.tile([P, ACTIONS], F32, tag="t1", name="t1")
-            nc.vector.tensor_tensor(out=t1[:], in0=pb_of.pop(s)[:], in1=eps_rows[:], op=MULT)
-            t2 = epi.tile([P, ACTIONS], F32, tag="t2", name="t2")
-            nc.gpsimd.tensor_tensor(out=t2[:], in0=t1[:], in1=bias_rows[:], op=ADD)
-            t1_of[s] = t2
-
-        by_tile = out.rearrange("i (h s) a -> s (i h) a", h=H)
-
-        def finish(s):
-            o = epi.tile([P, ACTIONS], F32, tag="o", name="o")
-            nc.vector.tensor_tensor(out=o[:], in0=pa_of.pop(s)[:], in1=t1_of.pop(s)[:], op=ADD)
-            nc.sync.dma_start(out=by_tile[s], in_=o[:])
-
-        zmul(0, 1, 0)
-        zmul(0, 1, 1)
-        quant(0, 1, split=True)
-        mm_noise(0)
-        mm_prior(0)
-        zmul(1, 1, 0)
-        zmul(1, 1, 1)
-        zmul(2, 2, 0)
-        quant(1, 1)
-        mm_noise(1)
-        mm_prior(1)
-        zmul(2, 2, 1)
-        noise(0)
-        quant(2, 2)
-        mm_noise(2)
-        mm_prior(2)
-        mm_noise(3)
-        mm_prior(3)
-        noise(1)
-        zmul(4, 2, 0)
+        zmul(0, 0)
+        quant(0, 0)
+        noise_banks = []
+        sum_banks = []
+        for at in range(AT):
+            noise_banks.append(bank())
+            mm_turned(noise_banks[at], 2, 0, at, 0, True, False)
+        for at in range(AT):
+            sum_banks.append(bank())
+            mm_turned(sum_banks[at], 1, 0, at, 0, True, False)
+        zmul(0, 1)
+        quant(0, 1)
+        for at in range(AT):
+            mm_turned(noise_banks[at], 2, 0, at, 1, False, True)
+        for at in range(AT):
+            mm_turned(sum_banks[at], 1, 0, at, 1, False, False)
         quantize_w3(0)
-        zmul(4, 2, 1)
-        noise(2)
-        quant(4, 2)
-        noise(3)
+        for at in range(AT):
+            mm_turned(sum_banks[at], 3, 0, at, 0, False, False)
+        zmul(1, 0)
+        interleave_w3(nc.vector.tensor_copy, 1, 1)
+        quant(1, 0)
         quantize_w3(1)
-        for p in range(TILES // 2):
-            a, b = 2 * p, 2 * p + 1
-            more_z = p + 3 < TILES // 2
-            more_mm = p + 2 < TILES // 2
-            mm_mean(a)
-            mm_mean(b)
-            if more_mm:
-                mm_noise(a + 4)
-                mm_noise(b + 4)
-            if more_z:
-                zmul(a + 6, 2, 0)
-            finish(a)
-            if more_z:
-                zmul(a + 6, 2, 1)
-            finish(b)
-            if more_z:
-                quant(a + 6, 2)
-            if more_mm:
-                mm_prior(a + 4)
-                mm_prior(b + 4)
-                noise(a + 4)
-                noise(b + 4)
+        for at in range(AT):
+            mm_turned(sum_banks[at], 3, 0, at, 1, False, True)
+        zmul(1, 1)
+        for at in range(AT):
+            noise = scale_noise(0, at, noise_banks[at])
+            add_up(0, at, sum_banks[at], noise)
+            if at == 0:
+                quant(1, 1)
+
+        for b in range(1, LAST):
+            for at in range(AT):
+                nb = bank()
+                sb = bank()
+                for g in range(G):
+                    mm_turned(nb, 2, b, at, g, g == 0, g == G - 1)
+                for g in range(G):
+                    mm_turned(sb, 1, b, at, g, g == 0, False)
+                for g in range(G):
+                    mm_turned(sb, 3, b, at, g, False, g == G - 1)
+                noise = scale_noise(b, at, nb)
+                add_up(b, at, sb, noise)
+                if at == 0:
+                    store(b - 1, turn_back(b - 1))
+                if at < G:
+                    zmul(b + 1, at)
+                else:
+                    quant(b + 1, at - G)
+
+        by_tile = out.rearrange("(b i) (h s) a -> b s (i h) a", b=BLOCKS, s=RT)[LAST]
+        noises = []
+        for s in range(RT):
+            nb = bank()
+            for g in range(G):
+                mm_rows(nb, 2, s, g, g == 0, g == G - 1)
+            t = epi.tile([P, ACTIONS], F32, tag="noise", name="noise")
+            nc.vector.tensor_tensor(out=t[:], in0=nb[:], in1=eps_rows[:], op=MULT)
+            noises.append(t)
+            if s == 1:
+                store(LAST - 1, turn_back(LAST - 1))
+        biased = []
+        for s in range(RT):
+            t = epi.tile([P, ACTIONS], F32, tag="biased", name="biased")
+            nc.vector.tensor_tensor(out=t[:], in0=noises[s][:], in1=bias_rows[:], op=ADD)
+            biased.append(t)
+        for s in range(RT):
+            sb = bank()
+            for g in range(G):
+                mm_rows(sb, 1, s, g, g == 0, False)
+            for g in range(G):
+                mm_rows(sb, 3, s, g, False, g == G - 1)
+            o = epi.tile([P, ACTIONS], F32, tag="o", name="o")
+            nc.vector.tensor_tensor(out=o[:], in0=sb[:], in1=biased[s][:], op=ADD)
+            nc.sync.dma_start(out=by_tile[s], in_=o[:])

@@ -24,8 +24,10 @@ BLOCKS = STATES * FRACTIONS // ROWS
 BS = STATES // BLOCKS
 AT = ACTIONS // P
 RT = ROWS // P
-H = P // BS
-LAST = BLOCKS - 1
+TURNED = 2
+RSTATES = STATES - BS * TURNED
+RTILES = RSTATES * FRACTIONS // P
+H = P // RSTATES
 
 
 def tile_implicit_quantile_head_s10_kernel(
@@ -58,8 +60,10 @@ def tile_implicit_quantile_head_s10_kernel(
         bias_rows = keep.tile([P, ACTIONS], BF16, align_bytes=64, name="bias_rows")
         ident = keep.tile([P, P], F32, align_bytes=64, name="ident")
         ident_b = keep.tile([P, P], BF16, align_bytes=64, name="ident_b")
-        psi_t = keep.tile([P, G, STATES, 4], BF16, align_bytes=64, name="psi_t")
+        psi_t = keep.tile([P, G, BS * TURNED, 4], BF16, align_bytes=64, name="psi_t")
         phi_t = keep.tile([P, G, FRACTIONS, 4], BF16, align_bytes=64, name="phi_t")
+        psi_r = keep.tile([P, G, RSTATES, H, 4], BF16, align_bytes=64, name="psi_r")
+        phi_r = keep.tile([P, G, RTILES, H, 4], BF16, align_bytes=64, name="phi_r")
         eps_t = keep.tile([P, AT, STATES + 1], F32, align_bytes=64, name="eps_t")
         warm = keep.tile([P, 1], F32, align_bytes=64, name="warm")
 
@@ -68,13 +72,14 @@ def tile_implicit_quantile_head_s10_kernel(
         nc.sync.dma_start(out=erows[0:STATES, :], in_=eps)
         nc.vector.memset(warm[:], 0.0)
         nc.scalar.activation(warm[:], warm[:], IDENTITY)
+        nc.vector.memset(erows[STATES:P, :].bitcast(I32), 0)
+        nc.gpsimd.dma_start(out=erows[STATES : STATES + 1, :], in_=bias.unsqueeze(0))
         nc.vector.memset(planes[:].rearrange("p a n -> p (a n)").bitcast(I32), 0)
         nc.vector.memset(rows[STATES + FRACTIONS : P, :].bitcast(I32), 0)
-        nc.vector.memset(erows[STATES:P, :].bitcast(I32), 0)
         make_identity(nc, ident[:])
-        make_identity(nc, ident_b[:])
         for h in range(H):
-            nc.gpsimd.dma_start(out=eps_rows[h:P:H, :], in_=eps[BS * LAST : STATES, :])
+            nc.gpsimd.dma_start(out=eps_rows[h:P:H, :], in_=eps[STATES - RSTATES : STATES, :])
+        nc.vector.tensor_copy(out=ident_b[:], in_=ident[:])
 
         def load_scales(src, at):
             by_row = src.rearrange("g (q r) n -> r q g n", r=4)
@@ -83,30 +88,33 @@ def tile_implicit_quantile_head_s10_kernel(
                     out=planes[r:P:32, at : at + G, :].bitcast(I32), in_=by_row[r].bitcast(I32)
                 )
 
-        nc.sync.dma_start(out=erows[STATES : STATES + 1, :], in_=bias.unsqueeze(0))
+        def load_w3(g):
+            nc.sync.dma_start(
+                out=w3_raw[:, g], in_=w3[512 * g : 512 * (g + 1), :].rearrange("(p j) n -> p j n", j=4)
+            )
+
         load_scales(w2_scales, G)
+        load_w3(0)
         nc.sync.dma_start(
             out=w2[:].bitcast(I32), in_=w2_words.rearrange("g p n t -> p g (n t)").bitcast(I32)
         )
         load_scales(w1_scales, 0)
         nc.sync.dma_start(out=w1[:].bitcast(I32), in_=w1_words.rearrange("g p b -> p g b").bitcast(I32))
-        for g in range(G):
-            nc.sync.dma_start(
-                out=w3_raw[:, g], in_=w3[512 * g : 512 * (g + 1), :].rearrange("(p j) n -> p j n", j=4)
-            )
+        load_w3(1)
         nc.sync.dma_start(out=bias_rows[:], in_=bias.partition_broadcast(P))
 
         words = rows[:].bitcast(F32)
+        pairs = []
         for g in range(G):
             turned = bank()
             for u in range(2):
                 nc.tensor.transpose(
                     turned[:, P * u : P * (u + 1)], words[:, 256 * g + u : 256 * (g + 1) : 2], ident[:]
                 )
-            pairs = turned[:, 0 : 2 * P].rearrange("p (u r) -> p r u", u=2)
+            pairs.append(turned[:, 0 : 2 * P].rearrange("p (u r) -> p r u", u=2))
             nc.scalar.copy(
                 out=psi_t[:, g].rearrange("p i t -> p (i t)").bitcast(F32).rearrange("p (i u) -> p i u", u=2),
-                in_=pairs[:, 0:STATES, :],
+                in_=pairs[g][:, 0 : BS * TURNED, :],
             )
             halves = turned[:, 0 : 2 * P].bitcast(BF16).rearrange("p (u r e) -> p r u e", u=2, e=2)
             nc.vector.tensor_scalar_max(
@@ -118,7 +126,11 @@ def tile_implicit_quantile_head_s10_kernel(
         eturned = psum.tile([P, AT, P], BF16, tag="bank", name="eturned")
         for at in range(AT):
             nc.tensor.transpose(eturned[:, at, :], erows[:, P * at : P * (at + 1)], ident_b[:])
-        nc.scalar.copy(out=eps_t[:], in_=eturned[:, :, 0 : STATES + 1])
+        for g in range(G):
+            nc.scalar.copy(
+                out=psi_r[:, g].rearrange("p i h t -> p (i h t)").bitcast(F32).rearrange("p (i h u) -> p i h u", h=H, u=2),
+                in_=pairs[g][:, BS * TURNED : STATES, :].unsqueeze(2).to_broadcast([P, RSTATES, H, 2]),
+            )
 
         def interleave_w3(copy, g, half):
             n = 256 * half
@@ -128,8 +140,10 @@ def tile_implicit_quantile_head_s10_kernel(
             )
 
         interleave_w3(nc.scalar.copy, 0, 0)
+        nc.scalar.copy(out=eps_t[:], in_=eturned[:, :, 0 : STATES + 1])
         interleave_w3(nc.scalar.copy, 0, 1)
         interleave_w3(nc.scalar.copy, 1, 0)
+        interleave_w3(nc.scalar.copy, 1, 1)
 
         def quantize_w3(g):
             nc.vector.quantize_mx(
@@ -143,24 +157,26 @@ def tile_implicit_quantile_head_s10_kernel(
         def zmul(b, g):
             z = zpool.tile([P, ROWS * 4], BF16, align_bytes=64, tag="z", name="z")
             z_of[b, g] = z
-            own = psi_t[:, g, BS * b : BS * (b + 1), :]
-            if b < LAST:
+            if b < TURNED:
                 shape = [P, BS, FRACTIONS, 4]
                 nc.vector.tensor_tensor(
                     out=z[:].rearrange("p (i j t) -> p i j t", j=FRACTIONS, t=4),
-                    in0=own.unsqueeze(2).to_broadcast(shape),
+                    in0=psi_t[:, g, BS * b : BS * (b + 1), :].unsqueeze(2).to_broadcast(shape),
                     in1=phi_t[:, g].unsqueeze(1).to_broadcast(shape),
                     op=MULT,
                 )
             else:
-                shape = [P, BS, H, 4]
-                for s in range(RT):
-                    nc.vector.tensor_tensor(
-                        out=z[:, 512 * s : 512 * (s + 1)].rearrange("p (i h t) -> p i h t", h=H, t=4),
-                        in0=own.unsqueeze(2).to_broadcast(shape),
-                        in1=phi_t[:, g, s:FRACTIONS:RT, :].unsqueeze(1).to_broadcast(shape),
-                        op=MULT,
-                    )
+                first = RT * (b - TURNED)
+                shape = [P, RT, RSTATES, H * 4]
+                nc.vector.tensor_tensor(
+                    out=z[:].rearrange("p (s i x) -> p s i x", s=RT, x=H * 4),
+                    in0=psi_r[:, g].rearrange("p i h t -> p i (h t)").unsqueeze(1).to_broadcast(shape),
+                    in1=phi_r[:, g, first : first + RT]
+                    .rearrange("p s h t -> p s (h t)")
+                    .unsqueeze(2)
+                    .to_broadcast(shape),
+                    op=MULT,
+                )
 
         def quant(b, g):
             if g == 0:
@@ -194,18 +210,34 @@ def tile_implicit_quantile_head_s10_kernel(
 
         def mm_rows(dst, kind, s, g, start, stop):
             w, ws = weights(kind, g)
+            b, r = TURNED + s // RT, s % RT
             nc.tensor.matmul_mx(
                 out=dst[:],
-                lhsT=codes_of[LAST][:, g, P * s : P * (s + 1)].bitcast(E4M3),
-                lhsT_scale=scales_of[LAST][:, g, P * s : P * (s + 1)],
+                lhsT=codes_of[b][:, g, P * r : P * (r + 1)].bitcast(E4M3),
+                lhsT_scale=scales_of[b][:, g, P * r : P * (r + 1)],
                 rhs=w,
                 rhs_scale=ws,
                 start=start,
                 stop=stop,
             )
 
-        def scale_noise(b, at, src):
+        noise_banks, sum_banks, noise_of, sums_of = {}, {}, {}, {}
+
+        def noise_turned(b, at):
+            noise_banks[b, at] = bank()
+            for g in range(G):
+                mm_turned(noise_banks[b, at], 2, b, at, g, g == 0, g == G - 1)
+
+        def sum_turned(b, at):
+            sum_banks[b, at] = bank()
+            for g in range(G):
+                mm_turned(sum_banks[b, at], 1, b, at, g, g == 0, False)
+            for g in range(G):
+                mm_turned(sum_banks[b, at], 3, b, at, g, False, g == G - 1)
+
+        def scale_noise(b, at):
             t = epi.tile([P, ROWS], F32, tag="noise", name="noise")
+            src = noise_banks[b, at]
             for i in range(BS):
                 nc.scalar.activation(
                     t[:, FRACTIONS * i : FRACTIONS * (i + 1)],
@@ -214,14 +246,14 @@ def tile_implicit_quantile_head_s10_kernel(
                     bias=eps_t[:, at, STATES : STATES + 1],
                     scale=eps_t[:, at, BS * b + i : BS * b + i + 1],
                 )
-            return t
+            noise_of[b, at] = t
 
-        sums_of = {}
-
-        def add_up(b, at, src, noise):
+        def add_up(b, at):
             if at == 0:
                 sums_of[b] = opool.tile([P, AT, ROWS], F32, tag="sums", name="sums")
-            nc.vector.tensor_tensor(out=sums_of[b][:, at, :], in0=src[:], in1=noise[:], op=ADD)
+            nc.vector.tensor_tensor(
+                out=sums_of[b][:, at, :], in0=sum_banks[b, at][:], in1=noise_of[b, at][:], op=ADD
+            )
 
         out_rows = out.rearrange("i j a -> (i j) a")
 
@@ -234,88 +266,106 @@ def tile_implicit_quantile_head_s10_kernel(
                         dst[:, P * at : P * (at + 1)], sums_of[b][:, at, P * r : P * (r + 1)], ident[:]
                     )
                 res.append(dst)
-            return res
-
-        def store(b, banks):
             for r in range(RT):
                 o = epi.tile([P, ACTIONS], F32, tag="o", name="o")
-                (nc.scalar.copy, nc.vector.tensor_copy)[r % 2](out=o[:], in_=banks[r][:])
+                nc.scalar.copy(out=o[:], in_=res[r][:])
                 lo = ROWS * b + P * r
                 nc.sync.dma_start(out=out_rows[lo : lo + P, :], in_=o[:])
 
+        by_tile = out[STATES - RSTATES : STATES].rearrange("i (h n) a -> n (i h) a", h=H)
+        biased_of = {}
+
+        def noise_rows(s):
+            noise_banks[s] = bank()
+            for g in range(G):
+                mm_rows(noise_banks[s], 2, s, g, g == 0, g == G - 1)
+
+        def finish_noise(s):
+            t = epi.tile([P, ACTIONS], F32, tag="noise", name="noise")
+            nc.vector.tensor_tensor(out=t[:], in0=noise_banks[s][:], in1=eps_rows[:], op=MULT)
+            biased_of[s] = epi.tile([P, ACTIONS], F32, tag="biased", name="biased")
+            nc.gpsimd.tensor_tensor(out=biased_of[s][:], in0=t[:], in1=bias_rows[:], op=ADD)
+
+        def sum_rows(s):
+            sum_banks[s] = bank()
+            for g in range(G):
+                mm_rows(sum_banks[s], 1, s, g, g == 0, False)
+            for g in range(G):
+                mm_rows(sum_banks[s], 3, s, g, False, g == G - 1)
+
+        def finish(s):
+            o = epi.tile([P, ACTIONS], F32, tag="o", name="o")
+            nc.vector.tensor_tensor(out=o[:], in0=sum_banks[s][:], in1=biased_of[s][:], op=ADD)
+            nc.sync.dma_start(out=by_tile[s], in_=o[:])
+
+        def share(banks, kind, g, start, stop):
+            for at in range(AT):
+                if start:
+                    banks[0, at] = bank()
+                mm_turned(banks[0, at], kind, 0, at, g, start, stop)
+
         zmul(0, 0)
         quant(0, 0)
-        noise_banks = []
-        sum_banks = []
-        for at in range(AT):
-            noise_banks.append(bank())
-            mm_turned(noise_banks[at], 2, 0, at, 0, True, False)
-        for at in range(AT):
-            sum_banks.append(bank())
-            mm_turned(sum_banks[at], 1, 0, at, 0, True, False)
+        share(noise_banks, 2, 0, True, False)
+        share(sum_banks, 1, 0, True, False)
         zmul(0, 1)
-        quant(0, 1)
-        for at in range(AT):
-            mm_turned(noise_banks[at], 2, 0, at, 1, False, True)
-        for at in range(AT):
-            mm_turned(sum_banks[at], 1, 0, at, 1, False, False)
+        for g in range(G):
+            nc.vector.tensor_copy(
+                out=phi_r[:, g], in_=phi_t[:, g].rearrange("p (h s) t -> p s h t", h=H)
+            )
         quantize_w3(0)
-        for at in range(AT):
-            mm_turned(sum_banks[at], 3, 0, at, 0, False, False)
+        share(sum_banks, 3, 0, False, False)
+        quant(0, 1)
+        share(noise_banks, 2, 1, False, True)
+        share(sum_banks, 1, 1, False, False)
         zmul(1, 0)
-        interleave_w3(nc.vector.tensor_copy, 1, 1)
-        quant(1, 0)
         quantize_w3(1)
-        for at in range(AT):
-            mm_turned(sum_banks[at], 3, 0, at, 1, False, True)
+        share(sum_banks, 3, 1, False, True)
+        quant(1, 0)
         zmul(1, 1)
-        for at in range(AT):
-            noise = scale_noise(0, at, noise_banks[at])
-            add_up(0, at, sum_banks[at], noise)
-            if at == 0:
-                quant(1, 1)
+        scale_noise(0, 0)
+        add_up(0, 0)
+        quant(1, 1)
+        for at in range(1, AT):
+            scale_noise(0, at)
+            add_up(0, at)
 
-        for b in range(1, LAST):
-            for at in range(AT):
-                nb = bank()
-                sb = bank()
-                for g in range(G):
-                    mm_turned(nb, 2, b, at, g, g == 0, g == G - 1)
-                for g in range(G):
-                    mm_turned(sb, 1, b, at, g, g == 0, False)
-                for g in range(G):
-                    mm_turned(sb, 3, b, at, g, False, g == G - 1)
-                noise = scale_noise(b, at, nb)
-                add_up(b, at, sb, noise)
-                if at == 0:
-                    store(b - 1, turn_back(b - 1))
-                if at < G:
-                    zmul(b + 1, at)
-                else:
-                    quant(b + 1, at - G)
-
-        by_tile = out.rearrange("(b i) (h s) a -> b s (i h) a", b=BLOCKS, s=RT)[LAST]
-        noises = []
-        for s in range(RT):
-            nb = bank()
-            for g in range(G):
-                mm_rows(nb, 2, s, g, g == 0, g == G - 1)
-            t = epi.tile([P, ACTIONS], F32, tag="noise", name="noise")
-            nc.vector.tensor_tensor(out=t[:], in0=nb[:], in1=eps_rows[:], op=MULT)
-            noises.append(t)
-            if s == 1:
-                store(LAST - 1, turn_back(LAST - 1))
-        biased = []
-        for s in range(RT):
-            t = epi.tile([P, ACTIONS], F32, tag="biased", name="biased")
-            nc.vector.tensor_tensor(out=t[:], in0=noises[s][:], in1=bias_rows[:], op=ADD)
-            biased.append(t)
-        for s in range(RT):
-            sb = bank()
-            for g in range(G):
-                mm_rows(sb, 1, s, g, g == 0, False)
-            for g in range(G):
-                mm_rows(sb, 3, s, g, False, g == G - 1)
-            o = epi.tile([P, ACTIONS], F32, tag="o", name="o")
-            nc.vector.tensor_tensor(out=o[:], in0=sb[:], in1=biased[s][:], op=ADD)
-            nc.sync.dma_start(out=by_tile[s], in_=o[:])
+        noise_turned(1, 0)
+        noise_turned(1, 1)
+        zmul(2, 0)
+        scale_noise(1, 0)
+        sum_turned(1, 0)
+        zmul(2, 1)
+        scale_noise(1, 1)
+        add_up(1, 0)
+        turn_back(0)
+        quant(2, 0)
+        noise_turned(1, 2)
+        sum_turned(1, 1)
+        quant(2, 1)
+        scale_noise(1, 2)
+        add_up(1, 1)
+        noise_turned(1, 3)
+        sum_turned(1, 2)
+        scale_noise(1, 3)
+        zmul(3, 0)
+        add_up(1, 2)
+        noise_rows(0)
+        sum_turned(1, 3)
+        zmul(3, 1)
+        add_up(1, 3)
+        noise_rows(1)
+        finish_noise(0)
+        quant(3, 0)
+        noise_rows(2)
+        finish_noise(1)
+        quant(3, 1)
+        turn_back(1)
+        finish_noise(2)
+        for s in range(RTILES):
+            sum_rows(s)
+            if s + 3 < RTILES:
+                noise_rows(s + 3)
+            finish(s)
+            if s + 3 < RTILES:
+                finish_noise(s + 3)

from contextlib import ExitStack

import concourse.mybir as mybir
from concourse.masks import make_identity

STATES, FRACTIONS, K, ACTIONS = 64, 32, 1024, 512
FLOPS = 3 * 2 * STATES * FRACTIONS * K * ACTIONS

F32 = mybir.dt.float32
BF16 = mybir.dt.bfloat16
U32 = mybir.dt.uint32
I32 = mybir.dt.int32
U8 = mybir.dt.uint8
E4M3 = mybir.dt.float8_e4m3fn_x4
E2M1 = mybir.dt.float4_e2m1fn_x4
ADD = mybir.AluOpType.add
MULT = mybir.AluOpType.mult
IDENTITY = mybir.ActivationFunctionType.Identity

P = 128
G = K // 512
ROWS = 512
BLOCKS = STATES * FRACTIONS // ROWS
BS = STATES // BLOCKS
AT = ACTIONS // P
RT = ROWS // P
TURNED = 2
RSTATES = STATES - BS * TURNED
RTILES = RSTATES * FRACTIONS // P
H = P // RSTATES


def tile_implicit_quantile_head_s10_kernel(
    tc, psi, emb, w1_words, w1_scales, w2_words, w2_scales, w3, eps, bias, out
):
    nc = tc.nc
    with ExitStack() as ctx:
        keep = ctx.enter_context(tc.tile_pool(name="keep", bufs=1))
        zpool = ctx.enter_context(tc.tile_pool(name="zpool", bufs=4))
        cpool = ctx.enter_context(tc.tile_pool(name="cpool", bufs=BLOCKS))
        epi = ctx.enter_context(tc.tile_pool(name="epi", bufs=5))
        opool = ctx.enter_context(tc.tile_pool(name="opool", bufs=2))
        psum = ctx.enter_context(tc.psum_pool(name="psum", bufs=8))
        ctx.enter_context(tc.manual_schedule())

        def bank():
            t = psum.tile([P, 512], F32, tag="bank", name="bank")
            return t

        rows = keep.tile([P, K], BF16, align_bytes=64, name="rows")
        erows = keep.tile([P, ACTIONS], BF16, align_bytes=64, name="erows")
        planes = keep.tile([P, 2 * G, ACTIONS], U8, align_bytes=64, name="planes")
        w2 = keep.tile([P, G, ACTIONS], U32, align_bytes=64, name="w2c")
        w1 = keep.tile([P, G, 2 * ACTIONS], U8, align_bytes=64, name="w1c")
        w3_raw = keep.tile([P, G, 4, ACTIONS], BF16, align_bytes=64, name="w3_raw")
        w3_grouped = keep.tile([P, G, ACTIONS, 4], BF16, align_bytes=64, name="w3_grouped")
        w3_codes = keep.tile([P, G, ACTIONS], U32, align_bytes=64, name="w3_codes")
        w3_scales = keep.tile([P, G, ACTIONS], U8, align_bytes=64, name="w3_scales")
        eps_rows = keep.tile([P, ACTIONS], BF16, align_bytes=64, name="eps_rows")
        bias_rows = keep.tile([P, ACTIONS], BF16, align_bytes=64, name="bias_rows")
        ident = keep.tile([P, P], F32, align_bytes=64, name="ident")
        ident_b = keep.tile([P, P], BF16, align_bytes=64, name="ident_b")
        psi_t = keep.tile([P, G, BS * TURNED, 4], BF16, align_bytes=64, name="psi_t")
        phi_t = keep.tile([P, G, FRACTIONS, 4], BF16, align_bytes=64, name="phi_t")
        psi_r = keep.tile([P, G, RSTATES, H, 4], BF16, align_bytes=64, name="psi_r")
        phi_r = keep.tile([P, G, RTILES, H, 4], BF16, align_bytes=64, name="phi_r")
        eps_t = keep.tile([P, AT, STATES + 1], F32, align_bytes=64, name="eps_t")
        warm = keep.tile([P, 1], F32, align_bytes=64, name="warm")

        nc.sync.dma_start(out=rows[0:STATES, :], in_=psi)
        nc.sync.dma_start(out=rows[STATES : STATES + FRACTIONS, :], in_=emb)
        nc.sync.dma_start(out=erows[0:STATES, :], in_=eps)
        nc.vector.memset(warm[:], 0.0)
        nc.scalar.activation(warm[:], warm[:], IDENTITY)
        nc.vector.memset(erows[STATES:P, :].bitcast(I32), 0)
        nc.gpsimd.dma_start(out=erows[STATES : STATES + 1, :], in_=bias.unsqueeze(0))
        nc.vector.memset(planes[:].rearrange("p a n -> p (a n)").bitcast(I32), 0)
        nc.vector.memset(rows[STATES + FRACTIONS : P, :].bitcast(I32), 0)
        make_identity(nc, ident[:])
        for h in range(H):
            nc.gpsimd.dma_start(out=eps_rows[h:P:H, :], in_=eps[STATES - RSTATES : STATES, :])
        nc.vector.tensor_copy(out=ident_b[:], in_=ident[:])

        def load_scales(src, at):
            by_row = src.rearrange("g (q r) n -> r q g n", r=4)
            for r in range(4):
                nc.sync.dma_start(
                    out=planes[r:P:32, at : at + G, :].bitcast(I32), in_=by_row[r].bitcast(I32)
                )

        def load_w3(g):
            nc.sync.dma_start(
                out=w3_raw[:, g], in_=w3[512 * g : 512 * (g + 1), :].rearrange("(p j) n -> p j n", j=4)
            )

        load_scales(w2_scales, G)
        load_w3(0)
        nc.sync.dma_start(
            out=w2[:].bitcast(I32), in_=w2_words.rearrange("g p n t -> p g (n t)").bitcast(I32)
        )
        load_scales(w1_scales, 0)
        nc.sync.dma_start(out=w1[:].bitcast(I32), in_=w1_words.rearrange("g p b -> p g b").bitcast(I32))
        load_w3(1)
        nc.sync.dma_start(out=bias_rows[:], in_=bias.partition_broadcast(P))

        words = rows[:].bitcast(F32)
        pairs = []
        for g in range(G):
            turned = bank()
            for u in range(2):
                nc.tensor.transpose(
                    turned[:, P * u : P * (u + 1)], words[:, 256 * g + u : 256 * (g + 1) : 2], ident[:]
                )
            pairs.append(turned[:, 0 : 2 * P].rearrange("p (u r) -> p r u", u=2))
            nc.scalar.copy(
                out=psi_t[:, g].rearrange("p i t -> p (i t)").bitcast(F32).rearrange("p (i u) -> p i u", u=2),
                in_=pairs[g][:, 0 : BS * TURNED, :],
            )
            halves = turned[:, 0 : 2 * P].bitcast(BF16).rearrange("p (u r e) -> p r u e", u=2, e=2)
            nc.vector.tensor_scalar_max(
                phi_t[:, g].rearrange("p j (u e) -> p j u e", e=2),
                halves[:, STATES : STATES + FRACTIONS, :, :],
                0.0,
            )

        eturned = psum.tile([P, AT, P], BF16, tag="bank", name="eturned")
        for at in range(AT):
            nc.tensor.transpose(eturned[:, at, :], erows[:, P * at : P * (at + 1)], ident_b[:])
        for g in range(G):
            nc.scalar.copy(
                out=psi_r[:, g].rearrange("p i h t -> p (i h t)").bitcast(F32).rearrange("p (i h u) -> p i h u", h=H, u=2),
                in_=pairs[g][:, BS * TURNED : STATES, :].unsqueeze(2).to_broadcast([P, RSTATES, H, 2]),
            )

        def interleave_w3(copy, g, half):
            n = 256 * half
            copy(
                out=w3_grouped[:, g, n : n + 256, :],
                in_=w3_raw[:, g, :, n : n + 256].rearrange("p j n -> p n j"),
            )

        interleave_w3(nc.scalar.copy, 0, 0)
        nc.scalar.copy(out=eps_t[:], in_=eturned[:, :, 0 : STATES + 1])
        interleave_w3(nc.scalar.copy, 0, 1)
        interleave_w3(nc.scalar.copy, 1, 0)
        interleave_w3(nc.scalar.copy, 1, 1)

        def quantize_w3(g):
            nc.vector.quantize_mx(
                out=w3_codes[:, g, :].bitcast(E4M3),
                scales=w3_scales[:, g, :],
                in_=w3_grouped[:, g].rearrange("p n t -> p (n t)"),
            )

        z_of, codes_of, scales_of = {}, {}, {}

        def zmul(b, g):
            z = zpool.tile([P, ROWS * 4], BF16, align_bytes=64, tag="z", name="z")
            z_of[b, g] = z
            if b < TURNED:
                shape = [P, BS, FRACTIONS, 4]
                nc.vector.tensor_tensor(
                    out=z[:].rearrange("p (i j t) -> p i j t", j=FRACTIONS, t=4),
                    in0=psi_t[:, g, BS * b : BS * (b + 1), :].unsqueeze(2).to_broadcast(shape),
                    in1=phi_t[:, g].unsqueeze(1).to_broadcast(shape),
                    op=MULT,
                )
            else:
                first = RT * (b - TURNED)
                shape = [P, RT, RSTATES, H * 4]
                nc.vector.tensor_tensor(
                    out=z[:].rearrange("p (s i x) -> p s i x", s=RT, x=H * 4),
                    in0=psi_r[:, g].rearrange("p i h t -> p i (h t)").unsqueeze(1).to_broadcast(shape),
                    in1=phi_r[:, g, first : first + RT]
                    .rearrange("p s h t -> p s (h t)")
                    .unsqueeze(2)
                    .to_broadcast(shape),
                    op=MULT,
                )

        def quant(b, g):
            if g == 0:
                codes_of[b] = cpool.tile([P, G, ROWS], U32, align_bytes=64, tag="codes", name="codes")
                scales_of[b] = cpool.tile([P, G, ROWS], U8, align_bytes=64, tag="scales", name="scales")
            nc.vector.quantize_mx(
                out=codes_of[b][:, g, :].bitcast(E4M3),
                scales=scales_of[b][:, g, :],
                in_=z_of.pop((b, g))[:],
            )

        def weights(kind, g, at=None):
            lo, hi = (0, ACTIONS) if at is None else (P * at, P * (at + 1))
            if kind == 1:
                return w1[:, g, 2 * lo : 2 * hi].bitcast(E2M1), planes[:, g, lo:hi]
            if kind == 2:
                return w2[:, g, lo:hi].bitcast(E4M3), planes[:, G + g, lo:hi]
            return w3_codes[:, g, lo:hi].bitcast(E4M3), w3_scales[:, g, lo:hi]

        def mm_turned(dst, kind, b, at, g, start, stop):
            w, ws = weights(kind, g, at)
            nc.tensor.matmul_mx(
                out=dst[:],
                lhsT=w,
                lhsT_scale=ws,
                rhs=codes_of[b][:, g, :].bitcast(E4M3),
                rhs_scale=scales_of[b][:, g, :],
                start=start,
                stop=stop,
            )

        def mm_rows(dst, kind, s, g, start, stop):
            w, ws = weights(kind, g)
            b, r = TURNED + s // RT, s % RT
            nc.tensor.matmul_mx(
                out=dst[:],
                lhsT=codes_of[b][:, g, P * r : P * (r + 1)].bitcast(E4M3),
                lhsT_scale=scales_of[b][:, g, P * r : P * (r + 1)],
                rhs=w,
                rhs_scale=ws,
                start=start,
                stop=stop,
            )

        noise_banks, sum_banks, noise_of, sums_of = {}, {}, {}, {}

        def noise_turned(b, at):
            noise_banks[b, at] = bank()
            for g in range(G):
                mm_turned(noise_banks[b, at], 2, b, at, g, g == 0, g == G - 1)

        def sum_turned(b, at):
            sum_banks[b, at] = bank()
            for g in range(G):
                mm_turned(sum_banks[b, at], 1, b, at, g, g == 0, False)
            for g in range(G):
                mm_turned(sum_banks[b, at], 3, b, at, g, False, g == G - 1)

        def scale_noise(b, at):
            t = epi.tile([P, ROWS], F32, tag="noise", name="noise")
            src = noise_banks[b, at]
            for i in range(BS):
                nc.scalar.activation(
                    t[:, FRACTIONS * i : FRACTIONS * (i + 1)],
                    src[:, FRACTIONS * i : FRACTIONS * (i + 1)],
                    IDENTITY,
                    bias=eps_t[:, at, STATES : STATES + 1],
                    scale=eps_t[:, at, BS * b + i : BS * b + i + 1],
                )
            noise_of[b, at] = t

        def add_up(b, at):
            if at == 0:
                sums_of[b] = opool.tile([P, AT, ROWS], F32, tag="sums", name="sums")
            nc.vector.tensor_tensor(
                out=sums_of[b][:, at, :], in0=sum_banks[b, at][:], in1=noise_of[b, at][:], op=ADD
            )

        out_rows = out.rearrange("i j a -> (i j) a")

        def turn_back(b):
            res = []
            for r in range(RT):
                dst = bank()
                for at in range(AT):
                    nc.tensor.transpose(
                        dst[:, P * at : P * (at + 1)], sums_of[b][:, at, P * r : P * (r + 1)], ident[:]
                    )
                res.append(dst)
            for r in range(RT):
                o = epi.tile([P, ACTIONS], F32, tag="o", name="o")
                nc.scalar.copy(out=o[:], in_=res[r][:])
                lo = ROWS * b + P * r
                nc.sync.dma_start(out=out_rows[lo : lo + P, :], in_=o[:])

        by_tile = out[STATES - RSTATES : STATES].rearrange("i (h n) a -> n (i h) a", h=H)
        biased_of = {}

        def noise_rows(s):
            noise_banks[s] = bank()
            for g in range(G):
                mm_rows(noise_banks[s], 2, s, g, g == 0, g == G - 1)

        def finish_noise(s):
            t = epi.tile([P, ACTIONS], F32, tag="noise", name="noise")
            nc.vector.tensor_tensor(out=t[:], in0=noise_banks[s][:], in1=eps_rows[:], op=MULT)
            biased_of[s] = epi.tile([P, ACTIONS], F32, tag="biased", name="biased")
            nc.gpsimd.tensor_tensor(out=biased_of[s][:], in0=t[:], in1=bias_rows[:], op=ADD)

        def sum_rows(s):
            sum_banks[s] = bank()
            for g in range(G):
                mm_rows(sum_banks[s], 1, s, g, g == 0, False)
            for g in range(G):
                mm_rows(sum_banks[s], 3, s, g, False, g == G - 1)

        def finish(s):
            o = epi.tile([P, ACTIONS], F32, tag="o", name="o")
            nc.vector.tensor_tensor(out=o[:], in0=sum_banks[s][:], in1=biased_of[s][:], op=ADD)
            nc.sync.dma_start(out=by_tile[s], in_=o[:])

        def share(banks, kind, g, start, stop):
            for at in range(AT):
                if start:
                    banks[0, at] = bank()
                mm_turned(banks[0, at], kind, 0, at, g, start, stop)

        zmul(0, 0)
        quant(0, 0)
        share(noise_banks, 2, 0, True, False)
        share(sum_banks, 1, 0, True, False)
        zmul(0, 1)
        for g in range(G):
            nc.vector.tensor_copy(
                out=phi_r[:, g], in_=phi_t[:, g].rearrange("p (h s) t -> p s h t", h=H)
            )
        quantize_w3(0)
        share(sum_banks, 3, 0, False, False)
        quant(0, 1)
        share(noise_banks, 2, 1, False, True)
        share(sum_banks, 1, 1, False, False)
        zmul(1, 0)
        quantize_w3(1)
        share(sum_banks, 3, 1, False, True)
        quant(1, 0)
        zmul(1, 1)
        scale_noise(0, 0)
        add_up(0, 0)
        quant(1, 1)
        for at in range(1, AT):
            scale_noise(0, at)
            add_up(0, at)

        noise_turned(1, 0)
        noise_turned(1, 1)
        zmul(2, 0)
        scale_noise(1, 0)
        sum_turned(1, 0)
        zmul(2, 1)
        scale_noise(1, 1)
        add_up(1, 0)
        turn_back(0)
        quant(2, 0)
        noise_turned(1, 2)
        sum_turned(1, 1)
        quant(2, 1)
        scale_noise(1, 2)
        add_up(1, 1)
        noise_turned(1, 3)
        sum_turned(1, 2)
        scale_noise(1, 3)
        zmul(3, 0)
        add_up(1, 2)
        noise_rows(0)
        sum_turned(1, 3)
        zmul(3, 1)
        add_up(1, 3)
        noise_rows(1)
        finish_noise(0)
        quant(3, 0)
        noise_rows(2)
        finish_noise(1)
        quant(3, 1)
        turn_back(1)
        finish_noise(2)
        for s in range(RTILES):
            sum_rows(s)
            if s + 3 < RTILES:
                noise_rows(s + 3)
            finish(s)
            if s + 3 < RTILES:
                finish_noise(s + 3)
